import numpy as np
import ml_dtypes


def mxq(x, axis, fmt="e4m3"):
    dtype, down = {"e4m3": (ml_dtypes.float8_e4m3fn, 7), "e5m2": (ml_dtypes.float8_e5m2, 14)}[fmt]
    v = np.moveaxis(np.asarray(x, np.float32).astype(ml_dtypes.bfloat16).astype(np.float64), axis, -1)
    blocks = v.reshape(v.shape[:-1] + (-1, 32))
    amax = np.abs(blocks).max(-1, keepdims=True)
    byte = np.maximum(np.where(amax > 0, np.frexp(amax)[1] - 1 + 127, 0) - down, 1)
    scale = np.exp2(byte - 127.0)
    codes = (blocks / scale).astype(np.float32).astype(dtype).astype(np.float64)
    return np.moveaxis((codes * scale).reshape(v.shape), -1, axis)


WIDE = False


def mx_kscale(k):
    if not WIDE:
        return np.ones(k)
    levels = np.array([10, -10, 5, -5, 0])
    if k % 512:
        return np.exp2(np.random.permutation(np.resize(levels, k // 32))).repeat(32)
    a = np.empty((k // 512, 16))
    for p in range(k // 512):
        a[p, :8] = np.random.permutation(np.resize(levels, 8))
        for g in range(8):
            far = levels[np.abs(levels - a[p, g]) >= 10]
            a[p, g + 8] = far[np.random.randint(len(far))]
    return np.exp2(a.ravel()).repeat(32)


def f64(x):
    return np.asarray(x).astype(np.float64)


def striped(idx):
    return np.tile(idx.reshape(-1, 16).T, (8, 1)).astype(np.uint16)


def unstriped(offs):
    return offs[:16].T.reshape(-1).astype(np.int64)


E2M1 = np.array([0.0, 0.5, 1.0, 1.5, 2.0, 3.0, 4.0, 6.0, -0.0, -0.5, -1.0, -1.5, -2.0, -3.0, -4.0, -6.0])


def pack_weight(w, fmt):
    k, n = w.shape
    w = f64(np.asarray(w, np.float32).astype(ml_dtypes.bfloat16)).reshape(k // 32, 32, n)
    amax = np.abs(w).max(1)
    if fmt == "e4m3":
        byte = np.frexp(amax)[1] - 1 + 127 - 7
    else:
        mant, ex = np.frexp(amax / 6.0)
        byte = np.where(mant > 0.5, ex, ex - 1) + 127
    byte = np.clip(np.where(amax > 0, byte, 1), 1, 254)
    scaled = (w * np.exp2(127.0 - byte)[:, None, :]).reshape(k, n).astype(np.float32)
    by_word = np.ascontiguousarray(scaled.reshape(k // 512, 128, 4, n).transpose(0, 1, 3, 2))
    if fmt == "e4m3":
        words = by_word.astype(ml_dtypes.float8_e4m3fn).view(np.uint8)
    else:
        c = by_word.astype(ml_dtypes.float4_e2m1fn).view(np.uint8) & 0xF
        words = (c[..., 0::2] | (c[..., 1::2] << 4)).reshape(k // 512, 128, 2 * n)
    return np.ascontiguousarray(words), np.ascontiguousarray(byte.astype(np.uint8).reshape(k // 512, 16, n))


def unpack_weight(words, scales, fmt):
    g, _, n = scales.shape
    words = np.ascontiguousarray(words).reshape(g, 128, n, -1)
    if fmt == "e4m3":
        vals = words.view(ml_dtypes.float8_e4m3fn).astype(np.float64)
    else:
        nib = np.empty((g, 128, n, 4), np.uint8)
        nib[..., 0::2] = words & 0xF
        nib[..., 1::2] = words >> 4
        vals = E2M1[nib]
    vals = vals * np.repeat(np.exp2(scales.astype(np.float64) - 127.0), 8, axis=1)[..., None]
    return vals.transpose(0, 1, 3, 2).reshape(g * 512, n)


def silu(v):
    return v / (1.0 + np.exp(-np.maximum(v, -700.0)))


K, T, E, C, H, N = 512, 512, 8, 128, 512, 256


def by_expert(wq, xq):
    return np.concatenate([wq[e].T @ xq[:, e * C:(e + 1) * C] for e in range(E)], axis=1)


def setup_inputs():
    n = np.random.standard_normal
    s = mx_kscale(K)[:, None]
    u = mx_kscale(H)
    first = np.random.permutation(np.repeat(np.arange(E), T // E))
    second = (first + 1 + np.random.permutation(np.repeat(np.arange(E - 1), -(-T // (E - 1)))[:T])) % E
    while np.bincount(second, minlength=E).max() != T // E:
        load = np.bincount(second, minlength=E); hi, lo = int(load.argmax()), int(load.argmin())
        t = np.flatnonzero((second == hi) & (first != lo))[0]; second[t] = lo
    slot_token = np.empty(E * C, np.int64); pos = np.empty((2, T), np.int64); fill = np.zeros(E, np.int64)
    place = np.stack([np.random.permutation(C) for _ in range(E)])
    for r, deal in enumerate((first, second)):
        for t in np.random.permutation(T):
            e = deal[t]; j = e * C + place[e, fill[e]]; fill[e] += 1; slot_token[j] = t; pos[r, t] = j
    g = np.random.uniform(0.2, 0.8, T)
    w1 = [pack_weight(m, "e2m1") for m in n((E + 1, K, H)) / np.sqrt(K) / s[None]]
    w3 = [pack_weight(m, "e2m1") for m in n((E + 1, K, H)) / np.sqrt(K) / s[None] * u[None, None, :]]
    w2 = [pack_weight(m, "e2m1") for m in n((E + 1, H, N)) / np.sqrt(H) / u[None, :, None]]
    x = pack_weight(n((K, T)) * s, "e4m3")
    return {
        "x_words": x[0],
        "x_scales": x[1],
        "w1_words": np.stack([m[0] for m in w1]),
        "w1_scales": np.stack([m[1] for m in w1]),
        "w3_words": np.stack([m[0] for m in w3]),
        "w3_scales": np.stack([m[1] for m in w3]),
        "w2_words": np.stack([m[0] for m in w2]),
        "w2_scales": np.stack([m[1] for m in w2]),
        "gate": np.stack([np.tile(g, (N, 1)), np.tile(1.0 - g, (N, 1))]).astype(np.float32),
        "offs": striped(slot_token),
        "pos1": striped(pos[0]),
        "pos2": striped(pos[1]),
    }


def reference(x_words, x_scales, w1_words, w1_scales, w3_words, w3_scales, w2_words, w2_scales, gate, offs, pos1, pos2):
    idx = unstriped(offs)
    w1 = np.stack([unpack_weight(w1_words[e], w1_scales[e], "e2m1") for e in range(E + 1)])
    w3 = np.stack([unpack_weight(w3_words[e], w3_scales[e], "e2m1") for e in range(E + 1)])
    w2 = np.stack([unpack_weight(w2_words[e], w2_scales[e], "e2m1") for e in range(E + 1)])
    w1q, w3q, w2q = w1, w3, w2
    xs = unpack_weight(x_words, x_scales, "e4m3")
    hs = silu(w1q[E].T @ xs) * (w3q[E].T @ xs)
    ys = w2q[E].T @ mxq(hs, 0, "e4m3")
    xq = unpack_weight(x_words, x_scales, "e4m3")[:, idx]
    h = silu(by_expert(w1q, xq))
    h = h * by_expert(w3q, xq)
    y = by_expert(w2q, mxq(h, 0, "e4m3"))
    return ys + f64(gate[0]) * y[:, unstriped(pos1)] + f64(gate[1]) * y[:, unstriped(pos2)]

@@ -1,0 +1,230 @@
+from contextlib import ExitStack
+
+import concourse.mybir as mybir
+from concourse.masks import make_identity
+
+K, T, E, C, H, N = 512, 512, 8, 128, 512, 256
+S = E * C
+FLOPS = 2 * (S + T) * (2 * K * H + H * N)
+
+F32 = mybir.dt.float32
+BF16 = mybir.dt.bfloat16
+I32 = mybir.dt.int32
+U32 = mybir.dt.uint32
+U16 = mybir.dt.uint16
+U8 = mybir.dt.uint8
+FP8X4 = mybir.dt.float8_e4m3fn_x4
+FP4X4 = mybir.dt.float4_e2m1fn_x4
+MULT = mybir.AluOpType.mult
+ADD = mybir.AluOpType.add
+SILU = mybir.ActivationFunctionType.Silu
+
+P = 128
+
+
+def tile_moe_shr_glu_silu_kernel(
+    tc, x_words, x_scales, w1_words, w1_scales, w3_words, w3_scales, w2_words, w2_scales, gate, offs, pos1, pos2, out
+):
+    nc = tc.nc
+    with ExitStack() as ctx:
+        keep = ctx.enter_context(tc.tile_pool(name="keep", bufs=1))
+        ring = ctx.enter_context(tc.tile_pool(name="ring", bufs=2))
+        psum = ctx.enter_context(tc.psum_pool(name="psum", bufs=1))
+
+        def plane(name, experts, width):
+            t = keep.tile([P, experts, width], U8, name=name, align_bytes=64)
+            nc.vector.memset(t[:].bitcast(I32), 0)
+            return t
+
+        def load_plane(t, scales, e0, e1):
+            for r in range(4):
+                nc.sync.dma_start(
+                    t[r:P:32, :, :].bitcast(I32),
+                    scales[e0:e1, 0, r:16:4, :].rearrange("e q i -> q e i").bitcast(I32),
+                )
+
+        def load_words(name, words, e0, e1):
+            t = keep.tile([P, e1 - e0, words.shape[3]], U8, name=name, align_bytes=64)
+            nc.sync.dma_start(t[:].bitcast(I32), words[e0:e1, 0].rearrange("e p b -> p e b").bitcast(I32))
+            return t
+
+        offs_t = keep.tile([P, S // 16], U16, name="offs_t")
+        pos1_t = keep.tile([P, T // 16], U16, name="pos1_t")
+        pos2_t = keep.tile([P, T // 16], U16, name="pos2_t")
+        xw = keep.tile([P, T], U32, name="xw", align_bytes=64)
+        xs = keep.tile([P, T], U8, name="xs", align_bytes=64)
+        ident = keep.tile([P, P], F32, name="ident", align_bytes=64)
+        make_identity(nc, ident[:])
+
+        nc.vector.memset(xs[:].bitcast(I32), 0)
+        s1a = plane("s1a", 3, H)
+        s3a = plane("s3a", 3, H)
+        s1b = plane("s1b", 6, H)
+        s3b = plane("s3b", 6, H)
+        s2 = plane("s2", 9, N)
+
+        nc.sync.dma_start(offs_t[:], offs)
+        nc.sync.dma_start(xw[:].bitcast(I32), x_words[0].rearrange("p n t -> p (n t)").bitcast(I32))
+        for r in range(4):
+            nc.sync.dma_start(xs[r:P:32, :].bitcast(I32), x_scales[0, r:16:4, :].bitcast(I32))
+        w1 = {}
+        w3 = {}
+        w2 = {}
+
+        def load_first(e0, e1):
+            a = load_words("w1_%d" % e0, w1_words, e0, e1)
+            b = load_words("w3_%d" % e0, w3_words, e0, e1)
+            for e in range(e0, e1):
+                w1[e] = a[:, e - e0, :]
+                w3[e] = b[:, e - e0, :]
+
+        def load_second(e0, e1):
+            a = load_words("w2_%d" % e0, w2_words, e0, e1)
+            for e in range(e0, e1):
+                w2[e] = a[:, e - e0, :]
+
+        load_first(8, 9)
+        load_plane(s1a, w1_scales, 6, 9)
+        load_plane(s3a, w3_scales, 6, 9)
+        load_first(6, 8)
+        load_plane(s1b, w1_scales, 0, 6)
+        load_plane(s3b, w3_scales, 0, 6)
+        load_first(4, 6)
+        load_plane(s2, w2_scales, 0, 9)
+        load_second(4, 9)
+        load_first(2, 4)
+        load_first(0, 2)
+        load_second(0, 4)
+        nc.sync.dma_start(pos1_t[:], pos1)
+        nc.sync.dma_start(pos2_t[:], pos2)
+        gates = keep.tile([P, 2, T], F32, name="gates")
+        nc.sync.dma_start(gates[:], gate[:, 0:P, :].rearrange("l p t -> p l t"))
+
+        def scale1(e):
+            return (s1a[:, e - 6, :], s3a[:, e - 6, :]) if e >= 6 else (s1b[:, e, :], s3b[:, e, :])
+
+        y = [keep.tile([P, S], F32, name="y%d" % nb) for nb in range(2)]
+
+        def gather_words(pair):
+            gw = keep.tile([P, 2 * C], U32, name="gw%d" % pair, align_bytes=64)
+            nc.vector.tensor_copy(gw[:], xw[:].indirect(offs_t[:, 16 * pair : 16 * pair + 16]))
+            return gw
+
+        def gather_scales(pair):
+            gs = ring.tile([P, 2 * C], U8, name="gs", align_bytes=64)
+            nc.vector.tensor_copy(gs[:], xs[:].indirect(offs_t[:, 16 * pair : 16 * pair + 16]))
+            return gs
+
+        def first_layer(e, words, scales, name, tag):
+            sa, sb = scale1(e)
+            pa = psum.tile([P, H], F32, name="pa", tag=tag)
+            pb = psum.tile([P, H], F32, name="pb", bufs=4)
+            nc.tensor.matmul_mx(pa[:], words.bitcast(FP8X4), scales, w1[e].bitcast(FP4X4), sa, start=True, stop=True)
+            nc.tensor.matmul_mx(pb[:], words.bitcast(FP8X4), scales, w3[e].bitcast(FP4X4), sb, start=True, stop=True)
+            act = ring.tile([P, 2, P, 2], F32, name="act", bufs=3)
+            nc.scalar.activation(act[:], pa[:].rearrange("p (m u e) -> p u m e", u=2, e=2), SILU)
+            h = keep.tile([P, H], BF16, name=name, align_bytes=64)
+            nc.vector.tensor_tensor(
+                h[:].rearrange("p (u m e) -> p u m e", u=2, e=2),
+                pb[:].rearrange("p (m u e) -> p u m e", u=2, e=2),
+                act[:],
+                MULT,
+            )
+            return h
+
+        def turn_and_quantise(hs, codes, scales, tag):
+            pt = psum.tile([P, 2, 2, P], F32, name="pt", tag=tag)
+            for b in range(2):
+                hw = hs[b][:].bitcast(F32)
+                for u in range(2):
+                    nc.tensor.transpose(pt[:, b, u, :], hw[:, u * P : (u + 1) * P], ident[:])
+            ht = ring.tile([P, 4 * 2 * P], BF16, name="ht", align_bytes=64)
+            nc.scalar.copy(
+                ht[:].bitcast(F32).rearrange("p (b s u) -> p b s u", b=2, u=2),
+                pt[:].rearrange("p b u s -> p b s u"),
+            )
+            nc.vector.quantize_mx(codes.bitcast(FP8X4), scales, ht[:])
+
+        def second_layer(pair, hc, hsc, tag):
+            py = psum.tile([P, 2, 2 * C], F32, name="py", tag=tag)
+            for nb in range(2):
+                for b in range(2):
+                    e = 2 * pair + b
+                    nc.tensor.matmul_mx(
+                        py[:, nb, b * C : (b + 1) * C],
+                        w2[e][:, nb * 2 * P : (nb + 1) * 2 * P].bitcast(FP4X4),
+                        s2[:, e, nb * P : (nb + 1) * P],
+                        hc[:, b * C : (b + 1) * C].bitcast(FP8X4),
+                        hsc[:, b * C : (b + 1) * C],
+                        start=True,
+                        stop=True,
+                    )
+            for nb in range(2):
+                nc.scalar.copy(y[nb][:, pair * 2 * C : (pair + 1) * 2 * C], py[:, nb, :])
+
+        sc = keep.tile([P, T], U32, name="sc", align_bytes=64)
+        ssc = keep.tile([P, T], U8, name="ssc", align_bytes=64)
+        pair_of = {1: 3, 2: 2, 3: 1, 4: 0}
+        half_of = {0: 0, 5: 1}
+        gw = {g: gather_words(pair_of[g]) for g in pair_of}
+        hs = {}
+        quant = {}
+
+        def stage_one(g):
+            tags = ("even%d" % (g % 2), "odd%d" % (g % 2))
+            if g in half_of:
+                hs[g] = []
+                for b in range(2):
+                    cols = slice((2 * half_of[g] + b) * P, (2 * half_of[g] + b + 1) * P)
+                    hs[g].append(first_layer(E, xw[:, cols], xs[:, cols], "h%d_%d" % (g, b), tags[b]))
+            else:
+                gs = gather_scales(pair_of[g])
+                hs[g] = [
+                    first_layer(2 * pair_of[g] + b, gw[g][:, b * C : (b + 1) * C], gs[:, b * C : (b + 1) * C], "h%d_%d" % (g, b), tags[b])
+                    for b in range(2)
+                ]
+
+        def stage_two(g):
+            if g in half_of:
+                cols = slice(half_of[g] * 2 * P, (half_of[g] + 1) * 2 * P)
+                quant[g] = (sc[:, cols], ssc[:, cols])
+            else:
+                hc = keep.tile([P, 2 * C], U32, name="hc%d" % g, align_bytes=64)
+                hsc = keep.tile([P, 2 * C], U8, name="hsc%d" % g, align_bytes=64)
+                quant[g] = (hc[:], hsc[:])
+            turn_and_quantise(hs[g], quant[g][0], quant[g][1], "even%d" % ((g + 1) % 2))
+
+        def stage_three(g):
+            second_layer(pair_of[g], quant[g][0], quant[g][1], "odd%d" % (g % 2))
+
+        for step in range(7):
+            if step < 6:
+                stage_one(step)
+            if step >= 1:
+                stage_two(step - 1)
+            if step - 2 in pair_of:
+                stage_three(step - 2)
+        ys = []
+        for nb in range(2):
+            acc = psum.tile([P, T], F32, name="pb", bufs=4)
+            nc.tensor.matmul_mx(
+                acc[:],
+                w2[E][:, nb * 2 * P : (nb + 1) * 2 * P].bitcast(FP4X4),
+                s2[:, E, nb * P : (nb + 1) * P],
+                sc[:].bitcast(FP8X4),
+                ssc[:],
+                start=True,
+                stop=True,
+            )
+            ys.append(acc[:])
+
+        t1 = [keep.tile([P, T], F32, name="t1_%d" % nb) for nb in range(2)]
+        t2 = [keep.tile([P, T], F32, name="t2_%d" % nb) for nb in range(2)]
+        u = [keep.tile([P, T], F32, name="u_%d" % nb) for nb in range(2)]
+        o = [keep.tile([P, T], F32, name="o_%d" % nb) for nb in range(2)]
+        for nb in range(2):
+            nc.vector.tensor_tensor(t1[nb][:], y[nb][:].indirect(pos1_t[:]), gates[:, 0, :], MULT)
+            nc.vector.tensor_tensor(t2[nb][:], y[nb][:].indirect(pos2_t[:]), gates[:, 1, :], MULT)
+            nc.vector.tensor_tensor(u[nb][:], ys[nb], t1[nb][:], ADD)
+            nc.vector.tensor_tensor(o[nb][:], u[nb][:], t2[nb][:], ADD)
+            nc.sync.dma_start(out[nb * P : (nb + 1) * P, :], o[nb][:])

@@ -20,6 +20,7 @@ ADD = mybir.AluOpType.add
 SILU = mybir.ActivationFunctionType.Silu
 
 P = 128
+EARLY = 5
 
 
 def tile_moe_shr_glu_silu_kernel(
@@ -31,9 +32,9 @@ def tile_moe_shr_glu_silu_kernel(
         ring = ctx.enter_context(tc.tile_pool(name="ring", bufs=2))
         psum = ctx.enter_context(tc.psum_pool(name="psum", bufs=1))
 
-        def plane(name, experts, width):
+        def plane(name, experts, width, eng):
             t = keep.tile([P, experts, width], U8, name=name, align_bytes=64)
-            nc.vector.memset(t[:].bitcast(I32), 0)
+            eng.memset(t[:].bitcast(I32), 0)
             return t
 
         def load_plane(t, scales, e0, e1):
@@ -54,177 +55,168 @@ def tile_moe_shr_glu_silu_kernel(
         xw = keep.tile([P, T], U32, name="xw", align_bytes=64)
         xs = keep.tile([P, T], U8, name="xs", align_bytes=64)
         ident = keep.tile([P, P], F32, name="ident", align_bytes=64)
+        nc.gpsimd.memset(xs[:].bitcast(I32), 0)
+        s1a = plane("s1a", EARLY, H, nc.vector)
+        s3a = plane("s3a", EARLY, H, nc.vector)
         make_identity(nc, ident[:])
+        s1b = plane("s1b", E + 1 - EARLY, H, nc.gpsimd)
+        s3b = plane("s3b", E + 1 - EARLY, H, nc.gpsimd)
+        s2 = plane("s2", E + 1, N, nc.gpsimd)
 
-        nc.vector.memset(xs[:].bitcast(I32), 0)
-        s1a = plane("s1a", 3, H)
-        s3a = plane("s3a", 3, H)
-        s1b = plane("s1b", 6, H)
-        s3b = plane("s3b", 6, H)
-        s2 = plane("s2", 9, N)
-
-        nc.sync.dma_start(offs_t[:], offs)
-        nc.sync.dma_start(xw[:].bitcast(I32), x_words[0].rearrange("p n t -> p (n t)").bitcast(I32))
-        for r in range(4):
-            nc.sync.dma_start(xs[r:P:32, :].bitcast(I32), x_scales[0, r:16:4, :].bitcast(I32))
         w1 = {}
         w3 = {}
         w2 = {}
 
-        def load_first(e0, e1):
-            a = load_words("w1_%d" % e0, w1_words, e0, e1)
-            b = load_words("w3_%d" % e0, w3_words, e0, e1)
+        def load_into(table, name, words, e0, e1):
+            a = load_words("%s_%d" % (name, e0), words, e0, e1)
             for e in range(e0, e1):
-                w1[e] = a[:, e - e0, :]
-                w3[e] = b[:, e - e0, :]
+                table[e] = a[:, e - e0, :]
 
-        def load_second(e0, e1):
-            a = load_words("w2_%d" % e0, w2_words, e0, e1)
-            for e in range(e0, e1):
-                w2[e] = a[:, e - e0, :]
-
-        load_first(8, 9)
-        load_plane(s1a, w1_scales, 6, 9)
-        load_plane(s3a, w3_scales, 6, 9)
-        load_first(6, 8)
-        load_plane(s1b, w1_scales, 0, 6)
-        load_plane(s3b, w3_scales, 0, 6)
-        load_first(4, 6)
-        load_plane(s2, w2_scales, 0, 9)
-        load_second(4, 9)
-        load_first(2, 4)
-        load_first(0, 2)
-        load_second(0, 4)
+        gates = keep.tile([P, 2, T], F32, name="gates")
+        nc.sync.dma_start(offs_t[:], offs)
+        for r in range(4):
+            (nc.sync if r < 1 else nc.scalar).dma_start(xs[r:P:32, :].bitcast(I32), x_scales[0, r:16:4, :].bitcast(I32))
+        nc.sync.dma_start(xw[:].bitcast(I32), x_words[0].rearrange("p n t -> p (n t)").bitcast(I32))
+        load_into(w1, "w1", w1_words, 6, 9)
+        load_into(w3, "w3", w3_words, 6, 9)
+        load_plane(s1a, w1_scales, E + 1 - EARLY, E + 1)
+        load_plane(s3a, w3_scales, E + 1 - EARLY, E + 1)
+        load_into(w1, "w1", w1_words, 4, 6)
+        load_into(w3, "w3", w3_words, 4, 6)
+        load_plane(s1b, w1_scales, 0, E + 1 - EARLY)
+        load_plane(s3b, w3_scales, 0, E + 1 - EARLY)
+        load_into(w1, "w1", w1_words, 2, 4)
+        load_into(w3, "w3", w3_words, 2, 4)
+        load_into(w1, "w1", w1_words, 0, 2)
+        load_into(w3, "w3", w3_words, 0, 2)
+        load_plane(s2, w2_scales, 0, E + 1)
+        load_into(w2, "w2", w2_words, 0, 9)
         nc.sync.dma_start(pos1_t[:], pos1)
         nc.sync.dma_start(pos2_t[:], pos2)
-        gates = keep.tile([P, 2, T], F32, name="gates")
         nc.sync.dma_start(gates[:], gate[:, 0:P, :].rearrange("l p t -> p l t"))
 
         def scale1(e):
-            return (s1a[:, e - 6, :], s3a[:, e - 6, :]) if e >= 6 else (s1b[:, e, :], s3b[:, e, :])
+            late = E + 1 - EARLY
+            return (s1a[:, e - late, :], s3a[:, e - late, :]) if e >= late else (s1b[:, e, :], s3b[:, e, :])
 
         y = [keep.tile([P, S], F32, name="y%d" % nb) for nb in range(2)]
 
-        def gather_words(pair):
-            gw = keep.tile([P, 2 * C], U32, name="gw%d" % pair, align_bytes=64)
-            nc.vector.tensor_copy(gw[:], xw[:].indirect(offs_t[:, 16 * pair : 16 * pair + 16]))
-            return gw
+        gw = keep.tile([P, S], U32, name="gw", align_bytes=64)
+        gs = keep.tile([P, S], U8, name="gs", align_bytes=64)
+        for e0, e1 in ((6, 8), (4, 6), (2, 4), (0, 2)):
+            lists = offs_t[:, e0 * C // 16 : e1 * C // 16]
+            nc.vector.tensor_copy(gw[:, e0 * C : e1 * C], xw[:].indirect(lists))
+            nc.vector.tensor_copy(gs[:, e0 * C : e1 * C], xs[:].indirect(lists))
 
-        def gather_scales(pair):
-            gs = ring.tile([P, 2 * C], U8, name="gs", align_bytes=64)
-            nc.vector.tensor_copy(gs[:], xs[:].indirect(offs_t[:, 16 * pair : 16 * pair + 16]))
-            return gs
+        hc = keep.tile([P, S + T], U32, name="hc", align_bytes=64)
+        hsc = keep.tile([P, S + T], U8, name="hsc", align_bytes=64)
+        groups = ((8, 9), (6, 7), (4, 5), (2, 3), (0, 1), (10, 11))
+        hs = {}
 
-        def first_layer(e, words, scales, name, tag):
-            sa, sb = scale1(e)
-            pa = psum.tile([P, H], F32, name="pa", tag=tag)
-            pb = psum.tile([P, H], F32, name="pb", bufs=4)
-            nc.tensor.matmul_mx(pa[:], words.bitcast(FP8X4), scales, w1[e].bitcast(FP4X4), sa, start=True, stop=True)
-            nc.tensor.matmul_mx(pb[:], words.bitcast(FP8X4), scales, w3[e].bitcast(FP4X4), sb, start=True, stop=True)
-            act = ring.tile([P, 2, P, 2], F32, name="act", bufs=3)
-            nc.scalar.activation(act[:], pa[:].rearrange("p (m u e) -> p u m e", u=2, e=2), SILU)
-            h = keep.tile([P, H], BF16, name=name, align_bytes=64)
-            nc.vector.tensor_tensor(
-                h[:].rearrange("p (u m e) -> p u m e", u=2, e=2),
-                pb[:].rearrange("p (m u e) -> p u m e", u=2, e=2),
-                act[:],
-                MULT,
-            )
-            return h
+        def stage_one(g, tags):
+            blocks = groups[g]
+            pa = [psum.tile([P, H], F32, name="pa", tag=tags[b]) for b in range(len(blocks))]
+            pb = [psum.tile([P, H], F32, name="pb", bufs=3) for b in blocks]
+            for acc, table, which in ((pa, w1, 0), (pb, w3, 1)):
+                for b, blk in enumerate(blocks):
+                    e = min(blk, E)
+                    words, scales = (gw, gs) if blk < E else (xw, xs)
+                    cols = slice((blk % E) * C, (blk % E + 1) * C)
+                    nc.tensor.matmul_mx(
+                        acc[b][:], words[:, cols].bitcast(FP8X4), scales[:, cols], table[e].bitcast(FP4X4), scale1(e)[which], start=True, stop=True
+                    )
+            for b, blk in enumerate(blocks):
+                act = ring.tile([P, 2, P, 2], F32, name="act", bufs=4)
+                nc.scalar.activation(act[:], pa[b][:].rearrange("p (m u e) -> p u m e", u=2, e=2), SILU)
+                h = keep.tile([P, H], BF16, name="h%d" % blk, align_bytes=64)
+                nc.vector.tensor_tensor(
+                    h[:].rearrange("p (u m e) -> p u m e", u=2, e=2),
+                    pb[b][:].rearrange("p (m u e) -> p u m e", u=2, e=2),
+                    act[:],
+                    MULT,
+                )
+                hs[blk] = h
 
-        def turn_and_quantise(hs, codes, scales, tag):
-            pt = psum.tile([P, 2, 2, P], F32, name="pt", tag=tag)
-            for b in range(2):
-                hw = hs[b][:].bitcast(F32)
+        def stage_two(g, tag, eng):
+            blocks = groups[g]
+            n = len(blocks)
+            pt = psum.tile([P, n, 2, P], F32, name="pt", tag=tag)
+            for b, blk in enumerate(blocks):
+                hw = hs[blk][:].bitcast(F32)
                 for u in range(2):
                     nc.tensor.transpose(pt[:, b, u, :], hw[:, u * P : (u + 1) * P], ident[:])
-            ht = ring.tile([P, 4 * 2 * P], BF16, name="ht", align_bytes=64)
-            nc.scalar.copy(
-                ht[:].bitcast(F32).rearrange("p (b s u) -> p b s u", b=2, u=2),
-                pt[:].rearrange("p b u s -> p b s u"),
-            )
-            nc.vector.quantize_mx(codes.bitcast(FP8X4), scales, ht[:])
+            ht = ring.tile([P, 4 * n * P], BF16, name="ht", align_bytes=64)
+            eng(ht[:].bitcast(F32).rearrange("p (b s u) -> p b s u", b=n, u=2), pt[:].rearrange("p b u s -> p b s u"))
+            cols = slice(blocks[0] * C, (blocks[-1] + 1) * C)
+            nc.vector.quantize_mx(hc[:, cols].bitcast(FP8X4), hsc[:, cols], ht[:])
 
-        def second_layer(pair, hc, hsc, tag):
-            py = psum.tile([P, 2, 2 * C], F32, name="py", tag=tag)
-            for nb in range(2):
-                for b in range(2):
-                    e = 2 * pair + b
-                    nc.tensor.matmul_mx(
-                        py[:, nb, b * C : (b + 1) * C],
-                        w2[e][:, nb * 2 * P : (nb + 1) * 2 * P].bitcast(FP4X4),
-                        s2[:, e, nb * P : (nb + 1) * P],
-                        hc[:, b * C : (b + 1) * C].bitcast(FP8X4),
-                        hsc[:, b * C : (b + 1) * C],
-                        start=True,
-                        stop=True,
-                    )
-            for nb in range(2):
-                nc.scalar.copy(y[nb][:, pair * 2 * C : (pair + 1) * 2 * C], py[:, nb, :])
+        def stage_three(nb, half, tag, eng):
+            experts = range(half * E // 2, (half + 1) * E // 2)
+            py = psum.tile([P, len(experts), C], F32, name="py", tag=tag)
+            for b, e in reversed(list(enumerate(experts))):
+                cols = slice(e * C, (e + 1) * C)
+                nc.tensor.matmul_mx(
+                    py[:, b, :],
+                    w2[e][:, nb * 2 * P : (nb + 1) * 2 * P].bitcast(FP4X4),
+                    s2[:, e, nb * P : (nb + 1) * P],
+                    hc[:, cols].bitcast(FP8X4),
+                    hsc[:, cols],
+                    start=True,
+                    stop=True,
+                )
+            eng(y[nb][:, half * S // 2 : (half + 1) * S // 2], py[:].rearrange("p e c -> p (e c)"))
 
-        sc = keep.tile([P, T], U32, name="sc", align_bytes=64)
-        ssc = keep.tile([P, T], U8, name="ssc", align_bytes=64)
-        pair_of = {1: 3, 2: 2, 3: 1, 4: 0}
-        half_of = {0: 0, 5: 1}
-        gw = {g: gather_words(pair_of[g]) for g in pair_of}
-        hs = {}
-        quant = {}
-
-        def stage_one(g):
-            tags = ("even%d" % (g % 2), "odd%d" % (g % 2))
-            if g in half_of:
-                hs[g] = []
-                for b in range(2):
-                    cols = slice((2 * half_of[g] + b) * P, (2 * half_of[g] + b + 1) * P)
-                    hs[g].append(first_layer(E, xw[:, cols], xs[:, cols], "h%d_%d" % (g, b), tags[b]))
-            else:
-                gs = gather_scales(pair_of[g])
-                hs[g] = [
-                    first_layer(2 * pair_of[g] + b, gw[g][:, b * C : (b + 1) * C], gs[:, b * C : (b + 1) * C], "h%d_%d" % (g, b), tags[b])
-                    for b in range(2)
-                ]
-
-        def stage_two(g):
-            if g in half_of:
-                cols = slice(half_of[g] * 2 * P, (half_of[g] + 1) * 2 * P)
-                quant[g] = (sc[:, cols], ssc[:, cols])
-            else:
-                hc = keep.tile([P, 2 * C], U32, name="hc%d" % g, align_bytes=64)
-                hsc = keep.tile([P, 2 * C], U8, name="hsc%d" % g, align_bytes=64)
-                quant[g] = (hc[:], hsc[:])
-            turn_and_quantise(hs[g], quant[g][0], quant[g][1], "even%d" % ((g + 1) % 2))
-
-        def stage_three(g):
-            second_layer(pair_of[g], quant[g][0], quant[g][1], "odd%d" % (g % 2))
-
-        for step in range(7):
-            if step < 6:
-                stage_one(step)
-            if step >= 1:
-                stage_two(step - 1)
-            if step - 2 in pair_of:
-                stage_three(step - 2)
+        on_scalar = nc.scalar.copy
+        on_vector = nc.vector.tensor_copy
+        stage_one(0, ("banka", "bankb",))
+        stage_one(1, ("bankc", "bankd",))
+        stage_two(0, "bankc", on_scalar)
+        stage_one(2, ("banka", "bankb",))
+        stage_two(1, "banka", on_scalar)
+        stage_one(3, ("bankc", "bankd",))
+        stage_two(2, "bankc", on_scalar)
+        stage_one(4, ("banka", "bankb",))
+        stage_two(3, "banka", on_scalar)
+        stage_one(5, ("bankc", "bankd",))
+        stage_two(4, "bankb", on_scalar)
+        stage_three(0, 1, "banke", on_vector)
+        stage_three(1, 1, "banka", on_scalar)
+        stage_two(5, "bankc", on_scalar)
+        stage_three(0, 0, "bankd", on_scalar)
+        stage_three(1, 0, "bankb", on_scalar)
         ys = []
         for nb in range(2):
-            acc = psum.tile([P, T], F32, name="pb", bufs=4)
+            acc = psum.tile([P, T], F32, name="ys", tag="bank" + "ea"[nb])
             nc.tensor.matmul_mx(
                 acc[:],
                 w2[E][:, nb * 2 * P : (nb + 1) * 2 * P].bitcast(FP4X4),
                 s2[:, E, nb * P : (nb + 1) * P],
-                sc[:].bitcast(FP8X4),
-                ssc[:],
+                hc[:, S:].bitcast(FP8X4),
+                hsc[:, S:],
                 start=True,
                 stop=True,
             )
             ys.append(acc[:])
 
-        t1 = [keep.tile([P, T], F32, name="t1_%d" % nb) for nb in range(2)]
-        t2 = [keep.tile([P, T], F32, name="t2_%d" % nb) for nb in range(2)]
+        t10 = keep.tile([P, T], F32, name="ends")
+        t20 = ring.tile([P, T], F32, name="ht", align_bytes=64)
+        t11 = ring.tile([P, T], F32, name="ht", align_bytes=64)
         u = [keep.tile([P, T], F32, name="u_%d" % nb) for nb in range(2)]
         o = [keep.tile([P, T], F32, name="o_%d" % nb) for nb in range(2)]
-        for nb in range(2):
-            nc.vector.tensor_tensor(t1[nb][:], y[nb][:].indirect(pos1_t[:]), gates[:, 0, :], MULT)
-            nc.vector.tensor_tensor(t2[nb][:], y[nb][:].indirect(pos2_t[:]), gates[:, 1, :], MULT)
-            nc.vector.tensor_tensor(u[nb][:], ys[nb], t1[nb][:], ADD)
-            nc.vector.tensor_tensor(o[nb][:], u[nb][:], t2[nb][:], ADD)
-            nc.sync.dma_start(out[nb * P : (nb + 1) * P, :], o[nb][:])
+        nc.vector.tensor_tensor(t10[:], y[0][:].indirect(pos1_t[:]), gates[:, 0, :], MULT)
+        nc.vector.tensor_tensor(t20[:], y[0][:].indirect(pos2_t[:]), gates[:, 1, :], MULT)
+        nc.vector.tensor_tensor(t11[:], y[1][:].indirect(pos1_t[:]), gates[:, 0, :], MULT)
+        nc.vector.tensor_tensor(u[0][:], ys[0], t10[:], ADD)
+        nc.vector.tensor_tensor(u[1][:], ys[1], t11[:], ADD)
+        nc.vector.tensor_tensor(o[0][:], u[0][:], t20[:], ADD)
+        nc.sync.dma_start(out[0:P, :], o[0][:])
+        t21 = keep.tile([P, T], F32, name="ends")
+        parts = 2
+        width = T // parts
+        for h in range(parts):
+            cols = slice(h * width, (h + 1) * width)
+            nc.vector.tensor_tensor(t21[:, cols], y[1][:].indirect(pos2_t[:, h * width // 16 : (h + 1) * width // 16]), gates[:, 1, cols], MULT)
+        for h in range(parts):
+            cols = slice(h * width, (h + 1) * width)
+            nc.vector.tensor_tensor(o[1][:, cols], u[1][:, cols], t21[:, cols], ADD)
+            nc.sync.dma_start(out[P : 2 * P, cols], o[1][:, cols])

@@ -44,6 +44,14 @@ def tile_moe_shr_glu_silu_kernel(
                     scales[e0:e1, 0, r:16:4, :].rearrange("e q i -> q e i").bitcast(I32),
                 )
 
+        def load_planes(planes, e0, e1):
+            for r in range(4):
+                for t, scales in zip(planes, (w1_scales, w3_scales)):
+                    nc.sync.dma_start(
+                        t[r:P:32, :, :].bitcast(I32),
+                        scales[e0:e1, 0, r:16:4, :].rearrange("e q i -> q e i").bitcast(I32),
+                    )
+
         def load_words(name, words, e0, e1):
             t = keep.tile([P, e1 - e0, words.shape[3]], U8, name=name, align_bytes=64)
             nc.sync.dma_start(t[:].bitcast(I32), words[e0:e1, 0].rearrange("e p b -> p e b").bitcast(I32))
@@ -78,8 +86,8 @@ def tile_moe_shr_glu_silu_kernel(
             (nc.sync if r < 1 else nc.scalar).dma_start(xs[r:P:32, :].bitcast(I32), x_scales[0, r:16:4, :].bitcast(I32))
         nc.sync.dma_start(xw[:].bitcast(I32), x_words[0].rearrange("p n t -> p (n t)").bitcast(I32))
         load_into(w1, "w1", w1_words, 6, 9)
-        load_into(w3, "w3", w3_words, 6, 9)
         load_plane(s1a, w1_scales, E + 1 - EARLY, E + 1)
+        load_into(w3, "w3", w3_words, 6, 9)
         load_plane(s3a, w3_scales, E + 1 - EARLY, E + 1)
         load_into(w1, "w1", w1_words, 4, 6)
         load_into(w3, "w3", w3_words, 4, 6)
@@ -151,7 +159,7 @@ def tile_moe_shr_glu_silu_kernel(
             nc.vector.quantize_mx(hc[:, cols].bitcast(FP8X4), hsc[:, cols], ht[:])
 
         def stage_three(nb, half, tag, eng):
-            experts = range(half * E // 2, (half + 1) * E // 2)
+            experts = range(*((4, 8), (2, 4), (0, 2))[half])
             py = psum.tile([P, len(experts), C], F32, name="py", tag=tag)
             for b, e in reversed(list(enumerate(experts))):
                 cols = slice(e * C, (e + 1) * C)
@@ -164,7 +172,7 @@ def tile_moe_shr_glu_silu_kernel(
                     start=True,
                     stop=True,
                 )
-            eng(y[nb][:, half * S // 2 : (half + 1) * S // 2], py[:].rearrange("p e c -> p (e c)"))
+            eng(y[nb][:, experts[0] * C : (experts[-1] + 1) * C], py[:].rearrange("p e c -> p (e c)"))
 
         on_scalar = nc.scalar.copy
         on_vector = nc.vector.tensor_copy
@@ -179,14 +187,16 @@ def tile_moe_shr_glu_silu_kernel(
         stage_two(3, "banka", on_scalar)
         stage_one(5, ("bankc", "bankd",))
         stage_two(4, "bankb", on_scalar)
-        stage_three(0, 1, "banke", on_vector)
-        stage_three(1, 1, "banka", on_scalar)
+        stage_three(0, 0, "banke", on_scalar)
+        stage_three(0, 1, "banka", on_vector)
+        stage_three(0, 2, "bankb", on_scalar)
+        stage_three(1, 0, "banke", on_scalar)
         stage_two(5, "bankc", on_scalar)
-        stage_three(0, 0, "bankd", on_scalar)
-        stage_three(1, 0, "bankb", on_scalar)
+        stage_three(1, 1, "bankd", on_scalar)
+        stage_three(1, 2, "banka", on_scalar)
         ys = []
         for nb in range(2):
-            acc = psum.tile([P, T], F32, name="ys", tag="bank" + "ea"[nb])
+            acc = psum.tile([P, T], F32, name="ys", tag="bank" + "be"[nb])
             nc.tensor.matmul_mx(
                 acc[:],
                 w2[E][:, nb * 2 * P : (nb + 1) * 2 * P].bitcast(FP4X4),

@@ -17,10 +17,20 @@ FP8X4 = mybir.dt.float8_e4m3fn_x4
 FP4X4 = mybir.dt.float4_e2m1fn_x4
 MULT = mybir.AluOpType.mult
 ADD = mybir.AluOpType.add
+COPY = mybir.ActivationFunctionType.Copy
 SILU = mybir.ActivationFunctionType.Silu
 
 P = 128
-EARLY = 5
+PER_COLUMN = 16
+ROW_BLOCKS = N // P
+TOKEN_BLOCKS = T // P
+SHARED = E
+ROUTED_PAIRS = tuple((e, e + 1) for e in range(E - 2, -1, -2))
+GROUPS = ((E, E + 1),) + ROUTED_PAIRS + ((E + 2, E + 3),)
+LATE = 4
+RANGES = ((4, 8), (2, 4), (0, 2))
+B_BANKS = 3
+ACT_BUFS = 4
 
 
 def tile_moe_shr_glu_silu_kernel(
@@ -32,201 +42,208 @@ def tile_moe_shr_glu_silu_kernel(
         ring = ctx.enter_context(tc.tile_pool(name="ring", bufs=2))
         psum = ctx.enter_context(tc.psum_pool(name="psum", bufs=1))
 
-        def plane(name, experts, width, eng):
-            t = keep.tile([P, experts, width], U8, name=name, align_bytes=64)
-            eng.memset(t[:].bitcast(I32), 0)
-            return t
+        def zeroed_plane(name, matrices, width, engine):
+            plane = keep.tile([P, matrices, width], U8, name=name, align_bytes=64)
+            engine.memset(plane[:].bitcast(I32), 0)
+            return plane
 
-        def load_plane(t, scales, e0, e1):
+        def load_plane(plane, scales, e0, e1):
             for r in range(4):
                 nc.sync.dma_start(
-                    t[r:P:32, :, :].bitcast(I32),
+                    plane[r:P:32, :, :].bitcast(I32),
                     scales[e0:e1, 0, r:16:4, :].rearrange("e q i -> q e i").bitcast(I32),
                 )
 
-        def load_planes(planes, e0, e1):
-            for r in range(4):
-                for t, scales in zip(planes, (w1_scales, w3_scales)):
-                    nc.sync.dma_start(
-                        t[r:P:32, :, :].bitcast(I32),
-                        scales[e0:e1, 0, r:16:4, :].rearrange("e q i -> q e i").bitcast(I32),
-                    )
+        def load_words(table, name, words, e0, e1):
+            tile = keep.tile([P, e1 - e0, words.shape[3]], U8, name="%s_%d" % (name, e0), align_bytes=64)
+            nc.sync.dma_start(tile[:].bitcast(I32), words[e0:e1, 0].rearrange("e p b -> p e b").bitcast(I32))
+            for e in range(e0, e1):
+                table[e] = tile[:, e - e0, :]
 
-        def load_words(name, words, e0, e1):
-            t = keep.tile([P, e1 - e0, words.shape[3]], U8, name=name, align_bytes=64)
-            nc.sync.dma_start(t[:].bitcast(I32), words[e0:e1, 0].rearrange("e p b -> p e b").bitcast(I32))
-            return t
-
-        offs_t = keep.tile([P, S // 16], U16, name="offs_t")
-        pos1_t = keep.tile([P, T // 16], U16, name="pos1_t")
-        pos2_t = keep.tile([P, T // 16], U16, name="pos2_t")
+        offs_t = keep.tile([P, S // PER_COLUMN], U16, name="offs_t")
+        pos1_t = keep.tile([P, T // PER_COLUMN], U16, name="pos1_t")
+        pos2_t = keep.tile([P, T // PER_COLUMN], U16, name="pos2_t")
         xw = keep.tile([P, T], U32, name="xw", align_bytes=64)
         xs = keep.tile([P, T], U8, name="xs", align_bytes=64)
         ident = keep.tile([P, P], F32, name="ident", align_bytes=64)
+
         nc.gpsimd.memset(xs[:].bitcast(I32), 0)
-        s1a = plane("s1a", EARLY, H, nc.vector)
-        s3a = plane("s3a", EARLY, H, nc.vector)
+        s1_head = zeroed_plane("s1_head", E + 1 - LATE, H, nc.vector)
+        s3_head = zeroed_plane("s3_head", E + 1 - LATE, H, nc.vector)
         make_identity(nc, ident[:])
-        s1b = plane("s1b", E + 1 - EARLY, H, nc.gpsimd)
-        s3b = plane("s3b", E + 1 - EARLY, H, nc.gpsimd)
-        s2 = plane("s2", E + 1, N, nc.gpsimd)
+        s1_late = zeroed_plane("s1_late", LATE, H, nc.gpsimd)
+        s3_late = zeroed_plane("s3_late", LATE, H, nc.gpsimd)
+        s2 = zeroed_plane("s2", E + 1, N, nc.gpsimd)
 
-        w1 = {}
-        w3 = {}
-        w2 = {}
-
-        def load_into(table, name, words, e0, e1):
-            a = load_words("%s_%d" % (name, e0), words, e0, e1)
-            for e in range(e0, e1):
-                table[e] = a[:, e - e0, :]
-
-        gates = keep.tile([P, 2, T], F32, name="gates")
+        w1, w3, w2 = {}, {}, {}
+        gate1_t = keep.tile([P, TOKEN_BLOCKS], F32, name="gate1_t")
+        gate2 = keep.tile([P, T], F32, name="gate2")
         nc.sync.dma_start(offs_t[:], offs)
         for r in range(4):
-            (nc.sync if r < 1 else nc.scalar).dma_start(xs[r:P:32, :].bitcast(I32), x_scales[0, r:16:4, :].bitcast(I32))
+            queue = nc.sync if r == 0 else nc.scalar
+            queue.dma_start(xs[r:P:32, :].bitcast(I32), x_scales[0, r:16:4, :].bitcast(I32))
         nc.sync.dma_start(xw[:].bitcast(I32), x_words[0].rearrange("p n t -> p (n t)").bitcast(I32))
-        load_into(w1, "w1", w1_words, 6, 9)
-        load_plane(s1a, w1_scales, E + 1 - EARLY, E + 1)
-        load_into(w3, "w3", w3_words, 6, 9)
-        load_plane(s3a, w3_scales, E + 1 - EARLY, E + 1)
-        load_into(w1, "w1", w1_words, 4, 6)
-        load_into(w3, "w3", w3_words, 4, 6)
-        load_plane(s1b, w1_scales, 0, E + 1 - EARLY)
-        load_plane(s3b, w3_scales, 0, E + 1 - EARLY)
-        load_into(w1, "w1", w1_words, 2, 4)
-        load_into(w3, "w3", w3_words, 2, 4)
-        load_into(w1, "w1", w1_words, 0, 2)
-        load_into(w3, "w3", w3_words, 0, 2)
+        load_words(w1, "w1", w1_words, ROUTED_PAIRS[0][0], E + 1)
+        load_plane(s1_head, w1_scales, LATE, E + 1)
+        load_words(w3, "w3", w3_words, ROUTED_PAIRS[0][0], E + 1)
+        load_plane(s3_head, w3_scales, LATE, E + 1)
+        for e0, e1 in ROUTED_PAIRS[1:]:
+            if e1 == LATE - 1:
+                load_plane(s1_late, w1_scales, 0, LATE)
+                load_plane(s3_late, w3_scales, 0, LATE)
+            load_words(w1, "w1", w1_words, e0, e1 + 1)
+            load_words(w3, "w3", w3_words, e0, e1 + 1)
         load_plane(s2, w2_scales, 0, E + 1)
-        load_into(w2, "w2", w2_words, 0, 9)
+        load_words(w2, "w2", w2_words, 0, E + 1)
         nc.sync.dma_start(pos1_t[:], pos1)
         nc.sync.dma_start(pos2_t[:], pos2)
-        nc.sync.dma_start(gates[:], gate[:, 0:P, :].rearrange("l p t -> p l t"))
+        with nc.allow_non_contiguous_dma(reason="one gate value a partition"):
+            nc.sync.dma_start(gate1_t[:], gate[0, 0, :].rearrange("(j p) -> p j", p=P))
+        nc.sync.dma_start(gate2[:], gate[1, 0:P, :])
 
-        def scale1(e):
-            late = E + 1 - EARLY
-            return (s1a[:, e - late, :], s3a[:, e - late, :]) if e >= late else (s1b[:, e, :], s3b[:, e, :])
+        def first_scales(e):
+            if e >= LATE:
+                return s1_head[:, e - LATE, :], s3_head[:, e - LATE, :]
+            return s1_late[:, e, :], s3_late[:, e, :]
 
-        y = [keep.tile([P, S], F32, name="y%d" % nb) for nb in range(2)]
+        y = [keep.tile([P, S], F32, name="y%d" % nb) for nb in range(ROW_BLOCKS)]
 
         gw = keep.tile([P, S], U32, name="gw", align_bytes=64)
         gs = keep.tile([P, S], U8, name="gs", align_bytes=64)
-        for e0, e1 in ((6, 8), (4, 6), (2, 4), (0, 2)):
-            lists = offs_t[:, e0 * C // 16 : e1 * C // 16]
-            nc.vector.tensor_copy(gw[:, e0 * C : e1 * C], xw[:].indirect(lists))
-            nc.vector.tensor_copy(gs[:, e0 * C : e1 * C], xs[:].indirect(lists))
+        for e0, e1 in ROUTED_PAIRS:
+            slots = slice(e0 * C, (e1 + 1) * C)
+            entries = offs_t[:, slots.start // PER_COLUMN : slots.stop // PER_COLUMN]
+            nc.vector.tensor_copy(gw[:, slots], xw[:].indirect(entries))
+            nc.vector.tensor_copy(gs[:, slots], xs[:].indirect(entries))
 
         hc = keep.tile([P, S + T], U32, name="hc", align_bytes=64)
         hsc = keep.tile([P, S + T], U8, name="hsc", align_bytes=64)
-        groups = ((8, 9), (6, 7), (4, 5), (2, 3), (0, 1), (10, 11))
-        hs = {}
+        h_tiles = {}
 
-        def stage_one(g, tags):
-            blocks = groups[g]
-            pa = [psum.tile([P, H], F32, name="pa", tag=tags[b]) for b in range(len(blocks))]
-            pb = [psum.tile([P, H], F32, name="pb", bufs=3) for b in blocks]
-            for acc, table, which in ((pa, w1, 0), (pb, w3, 1)):
-                for b, blk in enumerate(blocks):
-                    e = min(blk, E)
-                    words, scales = (gw, gs) if blk < E else (xw, xs)
-                    cols = slice((blk % E) * C, (blk % E + 1) * C)
+        def first_layer(blocks, a_banks):
+            pa = [psum.tile([P, H], F32, name="pa", tag=bank) for bank in a_banks]
+            pb = [psum.tile([P, H], F32, name="pb", bufs=B_BANKS) for block in blocks]
+            for which, (sums, table) in enumerate(((pa, w1), (pb, w3))):
+                for b, block in enumerate(blocks):
+                    e = min(block, SHARED)
+                    words, scales = (gw, gs) if block < E else (xw, xs)
+                    cols = slice(block % E * C, (block % E + 1) * C)
                     nc.tensor.matmul_mx(
-                        acc[b][:], words[:, cols].bitcast(FP8X4), scales[:, cols], table[e].bitcast(FP4X4), scale1(e)[which], start=True, stop=True
+                        sums[b][:],
+                        words[:, cols].bitcast(FP8X4),
+                        scales[:, cols],
+                        table[e].bitcast(FP4X4),
+                        first_scales(e)[which],
+                        start=True,
+                        stop=True,
                     )
-            for b, blk in enumerate(blocks):
-                act = ring.tile([P, 2, P, 2], F32, name="act", bufs=4)
+            for b, block in enumerate(blocks):
+                act = ring.tile([P, 2, P, 2], F32, name="act", bufs=ACT_BUFS)
                 nc.scalar.activation(act[:], pa[b][:].rearrange("p (m u e) -> p u m e", u=2, e=2), SILU)
-                h = keep.tile([P, H], BF16, name="h%d" % blk, align_bytes=64)
+                h = keep.tile([P, H], BF16, name="h%d" % block, align_bytes=64)
                 nc.vector.tensor_tensor(
                     h[:].rearrange("p (u m e) -> p u m e", u=2, e=2),
                     pb[b][:].rearrange("p (m u e) -> p u m e", u=2, e=2),
                     act[:],
                     MULT,
                 )
-                hs[blk] = h
+                h_tiles[block] = h
 
-        def stage_two(g, tag, eng):
-            blocks = groups[g]
-            n = len(blocks)
-            pt = psum.tile([P, n, 2, P], F32, name="pt", tag=tag)
-            for b, blk in enumerate(blocks):
-                hw = hs[blk][:].bitcast(F32)
+        def turn_and_quantise(blocks, bank):
+            pt = psum.tile([P, 2, 2, P], F32, name="pt", tag=bank)
+            for b, block in enumerate(blocks):
+                pairs = h_tiles[block][:].bitcast(F32)
                 for u in range(2):
-                    nc.tensor.transpose(pt[:, b, u, :], hw[:, u * P : (u + 1) * P], ident[:])
-            ht = ring.tile([P, 4 * n * P], BF16, name="ht", align_bytes=64)
-            eng(ht[:].bitcast(F32).rearrange("p (b s u) -> p b s u", b=n, u=2), pt[:].rearrange("p b u s -> p b s u"))
+                    nc.tensor.transpose(pt[:, b, u, :], pairs[:, u * P : (u + 1) * P], ident[:])
+            ht = ring.tile([P, 4 * 2 * C], BF16, name="ht", align_bytes=64)
+            nc.scalar.copy(
+                ht[:].bitcast(F32).rearrange("p (b s u) -> p b s u", b=2, u=2),
+                pt[:].rearrange("p b u s -> p b s u"),
+            )
             cols = slice(blocks[0] * C, (blocks[-1] + 1) * C)
             nc.vector.quantize_mx(hc[:, cols].bitcast(FP8X4), hsc[:, cols], ht[:])
 
-        def stage_three(nb, half, tag, eng):
-            experts = range(*((4, 8), (2, 4), (0, 2))[half])
-            py = psum.tile([P, len(experts), C], F32, name="py", tag=tag)
-            for b, e in reversed(list(enumerate(experts))):
-                cols = slice(e * C, (e + 1) * C)
+        def second_layer(nb, e0, e1, bank, copy_out):
+            py = psum.tile([P, e1 - e0, C], F32, name="py", tag=bank)
+            for e in reversed(range(e0, e1)):
+                slots = slice(e * C, (e + 1) * C)
                 nc.tensor.matmul_mx(
-                    py[:, b, :],
+                    py[:, e - e0, :],
                     w2[e][:, nb * 2 * P : (nb + 1) * 2 * P].bitcast(FP4X4),
                     s2[:, e, nb * P : (nb + 1) * P],
-                    hc[:, cols].bitcast(FP8X4),
-                    hsc[:, cols],
+                    hc[:, slots].bitcast(FP8X4),
+                    hsc[:, slots],
                     start=True,
                     stop=True,
                 )
-            eng(y[nb][:, experts[0] * C : (experts[-1] + 1) * C], py[:].rearrange("p e c -> p (e c)"))
+            copy_out(y[nb][:, e0 * C : e1 * C], py[:].rearrange("p e c -> p (e c)"))
 
-        on_scalar = nc.scalar.copy
-        on_vector = nc.vector.tensor_copy
-        stage_one(0, ("banka", "bankb",))
-        stage_one(1, ("bankc", "bankd",))
-        stage_two(0, "bankc", on_scalar)
-        stage_one(2, ("banka", "bankb",))
-        stage_two(1, "banka", on_scalar)
-        stage_one(3, ("bankc", "bankd",))
-        stage_two(2, "bankc", on_scalar)
-        stage_one(4, ("banka", "bankb",))
-        stage_two(3, "banka", on_scalar)
-        stage_one(5, ("bankc", "bankd",))
-        stage_two(4, "bankb", on_scalar)
-        stage_three(0, 0, "banke", on_scalar)
-        stage_three(0, 1, "banka", on_vector)
-        stage_three(0, 2, "bankb", on_scalar)
-        stage_three(1, 0, "banke", on_scalar)
-        stage_two(5, "bankc", on_scalar)
-        stage_three(1, 1, "bankd", on_scalar)
-        stage_three(1, 2, "banka", on_scalar)
-        ys = []
-        for nb in range(2):
-            acc = psum.tile([P, T], F32, name="ys", tag="bank" + "be"[nb])
-            nc.tensor.matmul_mx(
-                acc[:],
-                w2[E][:, nb * 2 * P : (nb + 1) * 2 * P].bitcast(FP4X4),
-                s2[:, E, nb * P : (nb + 1) * P],
-                hc[:, S:].bitcast(FP8X4),
-                hsc[:, S:],
-                start=True,
-                stop=True,
-            )
-            ys.append(acc[:])
+        pair_banks = (("bank_a", "bank_b"), ("bank_c", "bank_d"))
+        for g, blocks in enumerate(GROUPS):
+            first_layer(blocks, pair_banks[g % 2])
+            if 1 <= g < len(GROUPS) - 1:
+                turn_and_quantise(GROUPS[g - 1], pair_banks[g % 2][0])
 
-        t10 = keep.tile([P, T], F32, name="ends")
-        t20 = ring.tile([P, T], F32, name="ht", align_bytes=64)
-        t11 = ring.tile([P, T], F32, name="ht", align_bytes=64)
-        u = [keep.tile([P, T], F32, name="u_%d" % nb) for nb in range(2)]
-        o = [keep.tile([P, T], F32, name="o_%d" % nb) for nb in range(2)]
-        nc.vector.tensor_tensor(t10[:], y[0][:].indirect(pos1_t[:]), gates[:, 0, :], MULT)
-        nc.vector.tensor_tensor(t20[:], y[0][:].indirect(pos2_t[:]), gates[:, 1, :], MULT)
-        nc.vector.tensor_tensor(t11[:], y[1][:].indirect(pos1_t[:]), gates[:, 0, :], MULT)
-        nc.vector.tensor_tensor(u[0][:], ys[0], t10[:], ADD)
-        nc.vector.tensor_tensor(u[1][:], ys[1], t11[:], ADD)
-        nc.vector.tensor_tensor(o[0][:], u[0][:], t20[:], ADD)
-        nc.sync.dma_start(out[0:P, :], o[0][:])
-        t21 = keep.tile([P, T], F32, name="ends")
-        parts = 2
-        width = T // parts
-        for h in range(parts):
-            cols = slice(h * width, (h + 1) * width)
-            nc.vector.tensor_tensor(t21[:, cols], y[1][:].indirect(pos2_t[:, h * width // 16 : (h + 1) * width // 16]), gates[:, 1, cols], MULT)
-        for h in range(parts):
-            cols = slice(h * width, (h + 1) * width)
-            nc.vector.tensor_tensor(o[1][:, cols], u[1][:, cols], t21[:, cols], ADD)
-            nc.sync.dma_start(out[P : 2 * P, cols], o[1][:, cols])
+        tail_banks = ("bank_spare", "bank_b", "bank_a", "bank_c", "bank_d")
+        taken = []
+
+        def take_bank():
+            taken.append(tail_banks[len(taken) % len(tail_banks)])
+            return taken[-1]
+
+        for blocks in GROUPS[-2:]:
+            turn_and_quantise(blocks, take_bank())
+        for nb in range(ROW_BLOCKS):
+            for r, (e0, e1) in enumerate(RANGES):
+                copy_out = nc.vector.tensor_copy if (nb, r) == (0, 1) else nc.scalar.copy
+                second_layer(nb, e0, e1, take_bank(), copy_out)
+
+        ys_t = keep.tile([P, TOKEN_BLOCKS, N], F32, name="ys_t", align_bytes=64)
+        for j0 in range(0, TOKEN_BLOCKS, 2):
+            ps = psum.tile([P, 2, N], F32, name="ps", tag=take_bank())
+            for j in range(2):
+                cols = slice(S + (j0 + j) * P, S + (j0 + j + 1) * P)
+                nc.tensor.matmul_mx(
+                    ps[:, j, :],
+                    hc[:, cols].bitcast(FP8X4),
+                    hsc[:, cols],
+                    w2[SHARED].bitcast(FP4X4),
+                    s2[:, SHARED, :],
+                    start=True,
+                    stop=True,
+                )
+            nc.scalar.copy(ys_t[:, j0 : j0 + 2, :], ps[:])
+
+        first = [keep.tile([P, T], F32, name="first", tag="picked%d" % nb, align_bytes=64) for nb in range(ROW_BLOCKS)]
+        for nb in range(ROW_BLOCKS):
+            nc.vector.tensor_copy(first[nb][:], y[nb][:].indirect(pos1_t[:]))
+        turned = []
+        for nb in range(ROW_BLOCKS):
+            turned.append(psum.tile([P, TOKEN_BLOCKS, P], F32, name="turned", tag=take_bank()))
+            for j in range(TOKEN_BLOCKS):
+                nc.tensor.transpose(turned[nb][:, j, :], first[nb][:, j * P : (j + 1) * P], ident[:])
+        half = T // 2
+        partial = []
+        for nb in range(ROW_BLOCKS):
+            gated = keep.tile([P, TOKEN_BLOCKS, P], F32, name="gated%d" % nb, align_bytes=64)
+            for j in range(TOKEN_BLOCKS):
+                nc.scalar.activation(gated[:, j, :], turned[nb][:, j, :], COPY, scale=gate1_t[:, j : j + 1])
+            halves = [
+                psum.tile([P, half], F32, name="back", tag=take_bank()),
+                psum.tile([P, half], F32, name="back", tag="pb", bufs=B_BANKS),
+            ]
+            for j in range(TOKEN_BLOCKS):
+                dst = halves[j // 2][:, j % 2 * P : (j % 2 + 1) * P]
+                nc.tensor.matmul(dst, ys_t[:, j, nb * P : (nb + 1) * P], ident[:], start=True, stop=False, is_transpose=True)
+                nc.tensor.matmul(dst, gated[:, j, :], ident[:], start=False, stop=True, is_transpose=True)
+            partial.append(halves)
+
+        second = [keep.tile([P, T], F32, name="second", tag="picked%d" % nb, align_bytes=64) for nb in range(ROW_BLOCKS)]
+        for nb in range(ROW_BLOCKS):
+            nc.vector.tensor_tensor(second[nb][:], y[nb][:].indirect(pos2_t[:]), gate2[:], MULT)
+        for nb in range(ROW_BLOCKS):
+            result = keep.tile([P, T], F32, name="result%d" % nb)
+            for part in range(2):
+                tokens = slice(part * half, (part + 1) * half)
+                nc.vector.tensor_tensor(result[:, tokens], partial[nb][part][:], second[nb][:, tokens], ADD)
+                nc.sync.dma_start(out[nb * P : (nb + 1) * P, tokens], result[:, tokens])

from contextlib import ExitStack

import concourse.mybir as mybir
from concourse.masks import make_identity

K, T, E, C, H, N = 512, 512, 8, 128, 512, 256
S = E * C
FLOPS = 2 * (S + T) * (2 * K * H + H * N)

F32 = mybir.dt.float32
BF16 = mybir.dt.bfloat16
I32 = mybir.dt.int32
U32 = mybir.dt.uint32
U16 = mybir.dt.uint16
U8 = mybir.dt.uint8
FP8X4 = mybir.dt.float8_e4m3fn_x4
FP4X4 = mybir.dt.float4_e2m1fn_x4
MULT = mybir.AluOpType.mult
ADD = mybir.AluOpType.add
COPY = mybir.ActivationFunctionType.Copy
SILU = mybir.ActivationFunctionType.Silu

P = 128
PER_COLUMN = 16
ROW_BLOCKS = N // P
TOKEN_BLOCKS = T // P
SHARED = E
ROUTED_PAIRS = tuple((e, e + 1) for e in range(E - 2, -1, -2))
GROUPS = ((E, E + 1),) + ROUTED_PAIRS + ((E + 2, E + 3),)
LATE = 4
RANGES = ((4, 8), (2, 4), (0, 2))
B_BANKS = 3
ACT_BUFS = 4


def tile_moe_shr_glu_silu_kernel(
    tc, x_words, x_scales, w1_words, w1_scales, w3_words, w3_scales, w2_words, w2_scales, gate, offs, pos1, pos2, out
):
    nc = tc.nc
    with ExitStack() as ctx:
        keep = ctx.enter_context(tc.tile_pool(name="keep", bufs=1))
        ring = ctx.enter_context(tc.tile_pool(name="ring", bufs=2))
        psum = ctx.enter_context(tc.psum_pool(name="psum", bufs=1))

        def zeroed_plane(name, matrices, width, engine):
            plane = keep.tile([P, matrices, width], U8, name=name, align_bytes=64)
            engine.memset(plane[:].bitcast(I32), 0)
            return plane

        def load_plane(plane, scales, e0, e1):
            for r in range(4):
                nc.sync.dma_start(
                    plane[r:P:32, :, :].bitcast(I32),
                    scales[e0:e1, 0, r:16:4, :].rearrange("e q i -> q e i").bitcast(I32),
                )

        def load_words(table, name, words, e0, e1):
            tile = keep.tile([P, e1 - e0, words.shape[3]], U8, name="%s_%d" % (name, e0), align_bytes=64)
            nc.sync.dma_start(tile[:].bitcast(I32), words[e0:e1, 0].rearrange("e p b -> p e b").bitcast(I32))
            for e in range(e0, e1):
                table[e] = tile[:, e - e0, :]

        offs_t = keep.tile([P, S // PER_COLUMN], U16, name="offs_t")
        pos1_t = keep.tile([P, T // PER_COLUMN], U16, name="pos1_t")
        pos2_t = keep.tile([P, T // PER_COLUMN], U16, name="pos2_t")
        xw = keep.tile([P, T], U32, name="xw", align_bytes=64)
        xs = keep.tile([P, T], U8, name="xs", align_bytes=64)
        ident = keep.tile([P, P], F32, name="ident", align_bytes=64)

        nc.gpsimd.memset(xs[:].bitcast(I32), 0)
        s1_head = zeroed_plane("s1_head", E + 1 - LATE, H, nc.vector)
        s3_head = zeroed_plane("s3_head", E + 1 - LATE, H, nc.vector)
        make_identity(nc, ident[:])
        s1_late = zeroed_plane("s1_late", LATE, H, nc.gpsimd)
        s3_late = zeroed_plane("s3_late", LATE, H, nc.gpsimd)
        s2 = zeroed_plane("s2", E + 1, N, nc.gpsimd)

        w1, w3, w2 = {}, {}, {}
        gate1_t = keep.tile([P, TOKEN_BLOCKS], F32, name="gate1_t")
        gate2 = keep.tile([P, T], F32, name="gate2")
        nc.sync.dma_start(offs_t[:], offs)
        for r in range(4):
            queue = nc.sync if r == 0 else nc.scalar
            queue.dma_start(xs[r:P:32, :].bitcast(I32), x_scales[0, r:16:4, :].bitcast(I32))
        nc.sync.dma_start(xw[:].bitcast(I32), x_words[0].rearrange("p n t -> p (n t)").bitcast(I32))
        load_words(w1, "w1", w1_words, ROUTED_PAIRS[0][0], E + 1)
        load_plane(s1_head, w1_scales, LATE, E + 1)
        load_words(w3, "w3", w3_words, ROUTED_PAIRS[0][0], E + 1)
        load_plane(s3_head, w3_scales, LATE, E + 1)
        for e0, e1 in ROUTED_PAIRS[1:]:
            if e1 == LATE - 1:
                load_plane(s1_late, w1_scales, 0, LATE)
                load_plane(s3_late, w3_scales, 0, LATE)
            load_words(w1, "w1", w1_words, e0, e1 + 1)
            load_words(w3, "w3", w3_words, e0, e1 + 1)
        load_plane(s2, w2_scales, 0, E + 1)
        load_words(w2, "w2", w2_words, 0, E + 1)
        nc.sync.dma_start(pos1_t[:], pos1)
        nc.sync.dma_start(pos2_t[:], pos2)
        with nc.allow_non_contiguous_dma(reason="one gate value a partition"):
            nc.sync.dma_start(gate1_t[:], gate[0, 0, :].rearrange("(j p) -> p j", p=P))
        nc.sync.dma_start(gate2[:], gate[1, 0:P, :])

        def first_scales(e):
            if e >= LATE:
                return s1_head[:, e - LATE, :], s3_head[:, e - LATE, :]
            return s1_late[:, e, :], s3_late[:, e, :]

        y = [keep.tile([P, S], F32, name="y%d" % nb) for nb in range(ROW_BLOCKS)]

        gw = keep.tile([P, S], U32, name="gw", align_bytes=64)
        gs = keep.tile([P, S], U8, name="gs", align_bytes=64)
        for e0, e1 in ROUTED_PAIRS:
            slots = slice(e0 * C, (e1 + 1) * C)
            entries = offs_t[:, slots.start // PER_COLUMN : slots.stop // PER_COLUMN]
            nc.vector.tensor_copy(gw[:, slots], xw[:].indirect(entries))
            nc.vector.tensor_copy(gs[:, slots], xs[:].indirect(entries))

        hc = keep.tile([P, S + T], U32, name="hc", align_bytes=64)
        hsc = keep.tile([P, S + T], U8, name="hsc", align_bytes=64)
        h_tiles = {}

        def first_layer(blocks, a_banks):
            pa = [psum.tile([P, H], F32, name="pa", tag=bank) for bank in a_banks]
            pb = [psum.tile([P, H], F32, name="pb", bufs=B_BANKS) for block in blocks]
            for which, (sums, table) in enumerate(((pa, w1), (pb, w3))):
                for b, block in enumerate(blocks):
                    e = min(block, SHARED)
                    words, scales = (gw, gs) if block < E else (xw, xs)
                    cols = slice(block % E * C, (block % E + 1) * C)
                    nc.tensor.matmul_mx(
                        sums[b][:],
                        words[:, cols].bitcast(FP8X4),
                        scales[:, cols],
                        table[e].bitcast(FP4X4),
                        first_scales(e)[which],
                        start=True,
                        stop=True,
                    )
            for b, block in enumerate(blocks):
                act = ring.tile([P, 2, P, 2], F32, name="act", bufs=ACT_BUFS)
                nc.scalar.activation(act[:], pa[b][:].rearrange("p (m u e) -> p u m e", u=2, e=2), SILU)
                h = keep.tile([P, H], BF16, name="h%d" % block, align_bytes=64)
                nc.vector.tensor_tensor(
                    h[:].rearrange("p (u m e) -> p u m e", u=2, e=2),
                    pb[b][:].rearrange("p (m u e) -> p u m e", u=2, e=2),
                    act[:],
                    MULT,
                )
                h_tiles[block] = h

        def turn_and_quantise(blocks, bank):
            pt = psum.tile([P, 2, 2, P], F32, name="pt", tag=bank)
            for b, block in enumerate(blocks):
                pairs = h_tiles[block][:].bitcast(F32)
                for u in range(2):
                    nc.tensor.transpose(pt[:, b, u, :], pairs[:, u * P : (u + 1) * P], ident[:])
            ht = ring.tile([P, 4 * 2 * C], BF16, name="ht", align_bytes=64)
            nc.scalar.copy(
                ht[:].bitcast(F32).rearrange("p (b s u) -> p b s u", b=2, u=2),
                pt[:].rearrange("p b u s -> p b s u"),
            )
            cols = slice(blocks[0] * C, (blocks[-1] + 1) * C)
            nc.vector.quantize_mx(hc[:, cols].bitcast(FP8X4), hsc[:, cols], ht[:])

        def second_layer(nb, e0, e1, bank, copy_out):
            py = psum.tile([P, e1 - e0, C], F32, name="py", tag=bank)
            for e in reversed(range(e0, e1)):
                slots = slice(e * C, (e + 1) * C)
                nc.tensor.matmul_mx(
                    py[:, e - e0, :],
                    w2[e][:, nb * 2 * P : (nb + 1) * 2 * P].bitcast(FP4X4),
                    s2[:, e, nb * P : (nb + 1) * P],
                    hc[:, slots].bitcast(FP8X4),
                    hsc[:, slots],
                    start=True,
                    stop=True,
                )
            copy_out(y[nb][:, e0 * C : e1 * C], py[:].rearrange("p e c -> p (e c)"))

        pair_banks = (("bank_a", "bank_b"), ("bank_c", "bank_d"))
        for g, blocks in enumerate(GROUPS):
            first_layer(blocks, pair_banks[g % 2])
            if 1 <= g < len(GROUPS) - 1:
                turn_and_quantise(GROUPS[g - 1], pair_banks[g % 2][0])

        tail_banks = ("bank_spare", "bank_b", "bank_a", "bank_c", "bank_d")
        taken = []

        def take_bank():
            taken.append(tail_banks[len(taken) % len(tail_banks)])
            return taken[-1]

        for blocks in GROUPS[-2:]:
            turn_and_quantise(blocks, take_bank())
        for nb in range(ROW_BLOCKS):
            for r, (e0, e1) in enumerate(RANGES):
                copy_out = nc.vector.tensor_copy if (nb, r) == (0, 1) else nc.scalar.copy
                second_layer(nb, e0, e1, take_bank(), copy_out)

        ys_t = keep.tile([P, TOKEN_BLOCKS, N], F32, name="ys_t", align_bytes=64)
        for j0 in range(0, TOKEN_BLOCKS, 2):
            ps = psum.tile([P, 2, N], F32, name="ps", tag=take_bank())
            for j in range(2):
                cols = slice(S + (j0 + j) * P, S + (j0 + j + 1) * P)
                nc.tensor.matmul_mx(
                    ps[:, j, :],
                    hc[:, cols].bitcast(FP8X4),
                    hsc[:, cols],
                    w2[SHARED].bitcast(FP4X4),
                    s2[:, SHARED, :],
                    start=True,
                    stop=True,
                )
            nc.scalar.copy(ys_t[:, j0 : j0 + 2, :], ps[:])

        first = [keep.tile([P, T], F32, name="first", tag="picked%d" % nb, align_bytes=64) for nb in range(ROW_BLOCKS)]
        for nb in range(ROW_BLOCKS):
            nc.vector.tensor_copy(first[nb][:], y[nb][:].indirect(pos1_t[:]))
        turned = []
        for nb in range(ROW_BLOCKS):
            turned.append(psum.tile([P, TOKEN_BLOCKS, P], F32, name="turned", tag=take_bank()))
            for j in range(TOKEN_BLOCKS):
                nc.tensor.transpose(turned[nb][:, j, :], first[nb][:, j * P : (j + 1) * P], ident[:])
        half = T // 2
        partial = []
        for nb in range(ROW_BLOCKS):
            gated = keep.tile([P, TOKEN_BLOCKS, P], F32, name="gated%d" % nb, align_bytes=64)
            for j in range(TOKEN_BLOCKS):
                nc.scalar.activation(gated[:, j, :], turned[nb][:, j, :], COPY, scale=gate1_t[:, j : j + 1])
            halves = [
                psum.tile([P, half], F32, name="back", tag=take_bank()),
                psum.tile([P, half], F32, name="back", tag="pb", bufs=B_BANKS),
            ]
            for j in range(TOKEN_BLOCKS):
                dst = halves[j // 2][:, j % 2 * P : (j % 2 + 1) * P]
                nc.tensor.matmul(dst, ys_t[:, j, nb * P : (nb + 1) * P], ident[:], start=True, stop=False, is_transpose=True)
                nc.tensor.matmul(dst, gated[:, j, :], ident[:], start=False, stop=True, is_transpose=True)
            partial.append(halves)

        second = [keep.tile([P, T], F32, name="second", tag="picked%d" % nb, align_bytes=64) for nb in range(ROW_BLOCKS)]
        for nb in range(ROW_BLOCKS):
            nc.vector.tensor_tensor(second[nb][:], y[nb][:].indirect(pos2_t[:]), gate2[:], MULT)
        for nb in range(ROW_BLOCKS):
            result = keep.tile([P, T], F32, name="result%d" % nb)
            for part in range(2):
                tokens = slice(part * half, (part + 1) * half)
                nc.vector.tensor_tensor(result[:, tokens], partial[nb][part][:], second[nb][:, tokens], ADD)
                nc.sync.dma_start(out[nb * P : (nb + 1) * P, tokens], result[:, tokens])
